import numpy as np
import ml_dtypes

BF16 = ml_dtypes.bfloat16


def bf(x):
    return np.asarray(x, np.float32).astype(BF16)


def f32(x):
    return np.asarray(x, np.float32)


def f64(x):
    return np.asarray(x).astype(np.float64)


def striped(idx):
    return np.concatenate([l.reshape(-1, 16).T for l in idx])


def rows(idx, k):
    return np.tile(np.repeat(idx, 16, axis=0), (k // (16 * 8), 1))


def look(tab, idx):
    return np.take_along_axis(f64(tab), rows(idx, len(tab)), axis=1)


K, S, V, N = 256, 2048, 2048, 2048


def setup_inputs():
    return {"tab": f32(np.random.standard_normal((2, K, S))), "y": f32(np.random.standard_normal((K, V))), "offs": striped(np.stack([np.random.permutation(S)[:N] for _ in range(8)]))}


def reference(tab, y, offs):
    idx = np.stack([g.T.reshape(-1) for g in np.split(offs, 8)])
    x = (np.maximum(look(tab[0], idx), f64(y))) * (1.0 / (1.0 + np.exp(-look(tab[1], idx))))
    return x

@@ -1,0 +1,43 @@
+import concourse.mybir as mybir
+
+F32, U16 = mybir.dt.float32, mybir.dt.uint16
+ALU = mybir.AluOpType
+SIGMOID = mybir.ActivationFunctionType.Sigmoid
+
+P = 128
+GROUP = 16
+PIECE = 512
+
+
+def tile_lookup_vg_maxsig_out_kernel(tc, tab, y, offs, out):
+    nc = tc.nc
+    rows, places = tab.shape[1], tab.shape[2]
+    entries = y.shape[1]
+    blocks, pieces = rows // P, entries // PIECE
+    with (
+        tc.tile_pool(name="held", bufs=1) as held,
+        tc.tile_pool(name="work", bufs=blocks * pieces) as work,
+    ):
+        offsets = held.tile([P, entries // GROUP], U16, name="offsets")
+        nc.sync.dma_start(offsets[:], offs)
+        values, gates, stream = [], [], []
+        for b in range(blocks):
+            block = slice(b * P, (b + 1) * P)
+            values.append(held.tile([P, places], F32, name="values%d" % b))
+            gates.append(held.tile([P, places], F32, name="gates%d" % b))
+            stream.append(held.tile([P, entries], F32, name="stream%d" % b))
+            nc.sync.dma_start(values[b][:], tab[0, block, :])
+            nc.sync.dma_start(gates[b][:], tab[1, block, :])
+            nc.sync.dma_start(stream[b][:], y[block, :])
+        for b in range(blocks):
+            block = slice(b * P, (b + 1) * P)
+            for k in range(pieces):
+                cols = slice(k * PIECE, (k + 1) * PIECE)
+                picks = offsets[:, k * PIECE // GROUP : (k + 1) * PIECE // GROUP]
+                larger = work.tile([P, PIECE], F32, name="larger")
+                gate = work.tile([P, PIECE], F32, name="gate")
+                product = work.tile([P, PIECE], F32, name="product")
+                nc.vector.tensor_tensor(larger[:], values[b][:].indirect(picks), stream[b][:, cols], ALU.max)
+                nc.scalar.activation(gate[:], gates[b][:].indirect(picks), SIGMOID)
+                nc.vector.tensor_tensor(product[:], larger[:], gate[:], ALU.mult)
+                nc.sync.dma_start(out[block, cols], product[:])

@@ -7,6 +7,8 @@ SIGMOID = mybir.ActivationFunctionType.Sigmoid
 P = 128
 GROUP = 16
 PIECE = 512
+LAG = 2
+EARLY = 2
 
 
 def tile_lookup_vg_maxsig_out_kernel(tc, tab, y, offs, out):
@@ -14,30 +16,42 @@ def tile_lookup_vg_maxsig_out_kernel(tc, tab, y, offs, out):
     rows, places = tab.shape[1], tab.shape[2]
     entries = y.shape[1]
     blocks, pieces = rows // P, entries // PIECE
+    steps = [(b, k) for b in range(blocks) for k in range(pieces)]
     with (
         tc.tile_pool(name="held", bufs=1) as held,
-        tc.tile_pool(name="work", bufs=blocks * pieces) as work,
+        tc.tile_pool(name="work", bufs=len(steps)) as work,
+        tc.tile_pool(name="ring", bufs=LAG + 1) as ring,
     ):
         offsets = held.tile([P, entries // GROUP], U16, name="offsets")
         nc.sync.dma_start(offsets[:], offs)
-        values, gates, stream = [], [], []
+        values, gates, stream = [], [], {}
         for b in range(blocks):
             block = slice(b * P, (b + 1) * P)
             values.append(held.tile([P, places], F32, name="values%d" % b))
             gates.append(held.tile([P, places], F32, name="gates%d" % b))
-            stream.append(held.tile([P, entries], F32, name="stream%d" % b))
             nc.sync.dma_start(values[b][:], tab[0, block, :])
-            nc.sync.dma_start(gates[b][:], tab[1, block, :])
-            nc.sync.dma_start(stream[b][:], y[block, :])
-        for b in range(blocks):
-            block = slice(b * P, (b + 1) * P)
             for k in range(pieces):
-                cols = slice(k * PIECE, (k + 1) * PIECE)
-                picks = offsets[:, k * PIECE // GROUP : (k + 1) * PIECE // GROUP]
-                larger = work.tile([P, PIECE], F32, name="larger")
-                gate = work.tile([P, PIECE], F32, name="gate")
-                product = work.tile([P, PIECE], F32, name="product")
-                nc.vector.tensor_tensor(larger[:], values[b][:].indirect(picks), stream[b][:, cols], ALU.max)
-                nc.scalar.activation(gate[:], gates[b][:].indirect(picks), SIGMOID)
-                nc.vector.tensor_tensor(product[:], larger[:], gate[:], ALU.mult)
-                nc.sync.dma_start(out[block, cols], product[:])
+                if k == EARLY:
+                    nc.sync.dma_start(gates[b][:], tab[1, block, :])
+                stream[b, k] = work.tile([P, PIECE], F32, name="stream")
+                nc.sync.dma_start(stream[b, k][:], y[block, k * PIECE : (k + 1) * PIECE])
+
+        larger, gate = {}, {}
+
+        def look_up(b, k):
+            picks = offsets[:, k * PIECE // GROUP : (k + 1) * PIECE // GROUP]
+            larger[b, k] = ring.tile([P, PIECE], F32, name="larger")
+            gate[b, k] = work.tile([P, PIECE], F32, name="gate")
+            nc.vector.tensor_tensor(larger[b, k][:], values[b][:].indirect(picks), stream[b, k][:], ALU.max)
+            nc.scalar.activation(gate[b, k][:], gates[b][:].indirect(picks), SIGMOID)
+
+        def finish(b, k):
+            product = work.tile([P, PIECE], F32, name="product")
+            nc.vector.tensor_tensor(product[:], larger[b, k][:], gate[b, k][:], ALU.mult)
+            nc.sync.dma_start(out[b * P : (b + 1) * P, k * PIECE : (k + 1) * PIECE], product[:])
+
+        for i in range(len(steps) + LAG):
+            if i < len(steps):
+                look_up(*steps[i])
+            if i >= LAG:
+                finish(*steps[i - LAG])

@@ -22,6 +22,11 @@ def tile_lookup_vg_maxsig_out_kernel(tc, tab, y, offs, out):
         tc.tile_pool(name="work", bufs=len(steps)) as work,
         tc.tile_pool(name="ring", bufs=LAG + 1) as ring,
     ):
+        idle = held.tile([P, 8], F32, name="idle")
+        unread = held.tile([P, 8], F32, name="unread")
+        nc.vector.memset(idle[:], 0.0)
+        nc.scalar.activation(unread[:], idle[:], SIGMOID)
+
         offsets = held.tile([P, entries // GROUP], U16, name="offsets")
         nc.sync.dma_start(offsets[:], offs)
         values, gates, stream = [], [], {}

@@ -9,6 +9,7 @@ GROUP = 16
 PIECE = 512
 LAG = 2
 EARLY = 2
+LAST_PARTS = 2
 
 
 def tile_lookup_vg_maxsig_out_kernel(tc, tab, y, offs, out):
@@ -20,7 +21,6 @@ def tile_lookup_vg_maxsig_out_kernel(tc, tab, y, offs, out):
     with (
         tc.tile_pool(name="held", bufs=1) as held,
         tc.tile_pool(name="work", bufs=len(steps)) as work,
-        tc.tile_pool(name="ring", bufs=LAG + 1) as ring,
     ):
         idle = held.tile([P, 8], F32, name="idle")
         unread = held.tile([P, 8], F32, name="unread")
@@ -45,18 +45,22 @@ def tile_lookup_vg_maxsig_out_kernel(tc, tab, y, offs, out):
 
         def look_up(b, k):
             picks = offsets[:, k * PIECE // GROUP : (k + 1) * PIECE // GROUP]
-            larger[b, k] = ring.tile([P, PIECE], F32, name="larger")
+            larger[b, k] = work.tile([P, PIECE], F32, name="larger")
             gate[b, k] = work.tile([P, PIECE], F32, name="gate")
             nc.vector.tensor_tensor(larger[b, k][:], values[b][:].indirect(picks), stream[b, k][:], ALU.max)
             nc.scalar.activation(gate[b, k][:], gates[b][:].indirect(picks), SIGMOID)
 
-        def finish(b, k):
-            product = work.tile([P, PIECE], F32, name="product")
-            nc.vector.tensor_tensor(product[:], larger[b, k][:], gate[b, k][:], ALU.mult)
-            nc.sync.dma_start(out[b * P : (b + 1) * P, k * PIECE : (k + 1) * PIECE], product[:])
+        def finish(i):
+            b, k = steps[i]
+            product = stream[steps[(i + LAG) % len(steps)]]
+            width = PIECE // LAST_PARTS if i == len(steps) - 1 else PIECE
+            for c in range(0, PIECE, width):
+                part = slice(c, c + width)
+                nc.vector.tensor_tensor(product[:, part], larger[b, k][:, part], gate[b, k][:, part], ALU.mult)
+                nc.sync.dma_start(out[b * P : (b + 1) * P, k * PIECE + c : k * PIECE + c + width], product[:, part])
 
         for i in range(len(steps) + LAG):
             if i < len(steps):
                 look_up(*steps[i])
             if i >= LAG:
-                finish(*steps[i - LAG])
+                finish(i - LAG)

@@ -52,7 +52,7 @@ def tile_lookup_vg_maxsig_out_kernel(tc, tab, y, offs, out):
 
         def finish(i):
             b, k = steps[i]
-            product = stream[steps[(i + LAG) % len(steps)]]
+            product = stream[steps[(i + 1) % len(steps)]]
             width = PIECE // LAST_PARTS if i == len(steps) - 1 else PIECE
             for c in range(0, PIECE, width):
                 part = slice(c, c + width)

import concourse.mybir as mybir

F32, U16 = mybir.dt.float32, mybir.dt.uint16
ALU = mybir.AluOpType
SIGMOID = mybir.ActivationFunctionType.Sigmoid

P = 128
GROUP = 16
PIECE = 512
LAG = 2
EARLY = 2
LAST_PARTS = 2


def tile_lookup_vg_maxsig_out_kernel(tc, tab, y, offs, out):
    nc = tc.nc
    rows, places = tab.shape[1], tab.shape[2]
    entries = y.shape[1]
    blocks, pieces = rows // P, entries // PIECE
    steps = [(b, k) for b in range(blocks) for k in range(pieces)]
    with (
        tc.tile_pool(name="held", bufs=1) as held,
        tc.tile_pool(name="work", bufs=len(steps)) as work,
    ):
        idle = held.tile([P, 8], F32, name="idle")
        unread = held.tile([P, 8], F32, name="unread")
        nc.vector.memset(idle[:], 0.0)
        nc.scalar.activation(unread[:], idle[:], SIGMOID)

        offsets = held.tile([P, entries // GROUP], U16, name="offsets")
        nc.sync.dma_start(offsets[:], offs)
        values, gates, stream = [], [], {}
        for b in range(blocks):
            block = slice(b * P, (b + 1) * P)
            values.append(held.tile([P, places], F32, name="values%d" % b))
            gates.append(held.tile([P, places], F32, name="gates%d" % b))
            nc.sync.dma_start(values[b][:], tab[0, block, :])
            for k in range(pieces):
                if k == EARLY:
                    nc.sync.dma_start(gates[b][:], tab[1, block, :])
                stream[b, k] = work.tile([P, PIECE], F32, name="stream")
                nc.sync.dma_start(stream[b, k][:], y[block, k * PIECE : (k + 1) * PIECE])

        larger, gate = {}, {}

        def look_up(b, k):
            picks = offsets[:, k * PIECE // GROUP : (k + 1) * PIECE // GROUP]
            larger[b, k] = work.tile([P, PIECE], F32, name="larger")
            gate[b, k] = work.tile([P, PIECE], F32, name="gate")
            nc.vector.tensor_tensor(larger[b, k][:], values[b][:].indirect(picks), stream[b, k][:], ALU.max)
            nc.scalar.activation(gate[b, k][:], gates[b][:].indirect(picks), SIGMOID)

        def finish(i):
            b, k = steps[i]
            product = stream[steps[(i + 1) % len(steps)]]
            width = PIECE // LAST_PARTS if i == len(steps) - 1 else PIECE
            for c in range(0, PIECE, width):
                part = slice(c, c + width)
                nc.vector.tensor_tensor(product[:, part], larger[b, k][:, part], gate[b, k][:, part], ALU.mult)
                nc.sync.dma_start(out[b * P : (b + 1) * P, k * PIECE + c : k * PIECE + c + width], product[:, part])

        for i in range(len(steps) + LAG):
            if i < len(steps):
                look_up(*steps[i])
            if i >= LAG:
                finish(i - LAG)
